import numpy as np
import ml_dtypes


def mxq(x, axis, fmt="e4m3"):
    dtype, down = {"e4m3": (ml_dtypes.float8_e4m3fn, 7), "e5m2": (ml_dtypes.float8_e5m2, 14)}[fmt]
    v = np.moveaxis(np.asarray(x, np.float32).astype(ml_dtypes.bfloat16).astype(np.float64), axis, -1)
    blocks = v.reshape(v.shape[:-1] + (-1, 32))
    amax = np.abs(blocks).max(-1, keepdims=True)
    byte = np.maximum(np.where(amax > 0, np.frexp(amax)[1] - 1 + 127, 0) - down, 1)
    scale = np.exp2(byte - 127.0)
    codes = (blocks / scale).astype(np.float32).astype(dtype).astype(np.float64)
    return np.moveaxis((codes * scale).reshape(v.shape), -1, axis)


WIDE = False


def mx_kscale(k):
    if not WIDE:
        return np.ones(k)
    levels = np.array([10, -10, 5, -5, 0])
    if k % 512:
        return np.exp2(np.random.permutation(np.resize(levels, k // 32))).repeat(32)
    a = np.empty((k // 512, 16))
    for p in range(k // 512):
        a[p, :8] = np.random.permutation(np.resize(levels, 8))
        for g in range(8):
            far = levels[np.abs(levels - a[p, g]) >= 10]
            a[p, g + 8] = far[np.random.randint(len(far))]
    return np.exp2(a.ravel()).repeat(32)


BF16 = ml_dtypes.bfloat16


def bf(x):
    return np.asarray(x, np.float32).astype(BF16)


def f64(x):
    return np.asarray(x).astype(np.float64)


E2M1 = np.array([0.0, 0.5, 1.0, 1.5, 2.0, 3.0, 4.0, 6.0, -0.0, -0.5, -1.0, -1.5, -2.0, -3.0, -4.0, -6.0])


def pack_weight(w, fmt):
    k, n = w.shape
    w = f64(bf(w)).reshape(k // 32, 32, n)
    amax = np.abs(w).max(1)
    if fmt == "e4m3":
        byte = np.frexp(amax)[1] - 1 + 127 - 7
    else:
        mant, ex = np.frexp(amax / 6.0)
        byte = np.where(mant > 0.5, ex, ex - 1) + 127
    byte = np.clip(np.where(amax > 0, byte, 1), 1, 254)
    scaled = (w * np.exp2(127.0 - byte)[:, None, :]).reshape(k, n).astype(np.float32)
    by_word = np.ascontiguousarray(scaled.reshape(k // 512, 128, 4, n).transpose(0, 1, 3, 2))
    if fmt == "e4m3":
        words = by_word.astype(ml_dtypes.float8_e4m3fn).view(np.uint8)
    else:
        c = by_word.astype(ml_dtypes.float4_e2m1fn).view(np.uint8) & 0xF
        words = c[..., 0::2] | (c[..., 1::2] << 4)
    return np.ascontiguousarray(words), np.ascontiguousarray(byte.astype(np.uint8).reshape(k // 512, 16, n))


def unpack_weight(words, scales, fmt):
    g, p, n, _ = words.shape
    if fmt == "e4m3":
        vals = np.ascontiguousarray(words).view(ml_dtypes.float8_e4m3fn).astype(np.float64)
    else:
        nib = np.empty((g, p, n, 4), np.uint8)
        nib[..., 0::2] = words & 0xF
        nib[..., 1::2] = words >> 4
        vals = E2M1[nib]
    vals = vals * np.repeat(np.exp2(scales.astype(np.float64) - 127.0), 8, axis=1)[..., None]
    return vals.transpose(0, 1, 3, 2).reshape(g * 512, n)
def pack4(w):
    words, scales = pack_weight(w, "e2m1")
    return words.reshape(words.shape[0], 128, -1), scales


def unpack4(words, scales):
    return unpack_weight(words.reshape(words.shape[0], 128, -1, 2), scales, "e2m1")


def planes(Y):
    n, m = Y.shape
    b = f64(bf(Y)).reshape(n // 32, 32, m)
    amax = np.abs(b).max(1)
    byte = np.clip(np.where(amax > 0, np.frexp(amax)[1] - 1 + 127 - 7, 1), 1, 254)
    codes = (b * np.exp2(127.0 - byte)[:, None, :]).reshape(n, m).astype(np.float32).astype(ml_dtypes.float8_e4m3fn).view(np.uint8)
    words = codes.reshape(n // 512, 128, 4, m).transpose(0, 1, 3, 2)
    return np.ascontiguousarray(words), np.ascontiguousarray(byte.astype(np.uint8).reshape(n // 512, 16, m))


D, J, M = 2048, 1024, 1024


def setup_inputs():
    rnd = np.random.randn
    s = mx_kscale(D)
    t = mx_kscale(J)
    x_words, x_scales = pack_weight(rnd(D, M) / s[:, None], "e4m3")
    left = rnd(D, J) / np.sqrt(D)
    left_words, left_scales = pack4(left * s[:, None] * t[None, :])
    right = bf(rnd(J, D) / np.sqrt(J) / t[:, None])
    lam = bf(0.2 + 2.0 * np.random.rand(J))
    shift = bf(0.3 + np.random.rand(M))
    start = bf(0.5 * rnd(D, M))
    row_scale = bf(np.exp(0.8 * rnd(D)))
    return {"x_words": x_words, "x_scales": x_scales,
            "left_words": left_words, "left_scales": left_scales,
            "right": right, "lam": lam, "shift": shift,
            "start": start, "row_scale": row_scale}


def reference(x_words, x_scales, left_words, left_scales, right, lam, shift, start, row_scale):
    X = unpack_weight(x_words, x_scales, "e4m3")
    L = unpack4(left_words, left_scales)
    C = L.T @ X
    Z = C / (f64(lam)[:, None] + f64(shift)[None, :])
    V = mxq(f64(right), 0, "e4m3").T @ mxq(Z, 0, "e4m3")
    y = f64(row_scale)[:, None] * (f64(start) + V)
    words, scales = planes(y)
    return y, words, scales

from contextlib import ExitStack

import concourse.mybir as mybir
from concourse.masks import make_identity

D, J, M = 2048, 1024, 1024
FLOPS = 2 * D * J * M * 2

F32 = mybir.dt.float32
BF16 = mybir.dt.bfloat16
I32 = mybir.dt.int32
U32 = mybir.dt.uint32
U8 = mybir.dt.uint8
FP8X4 = mybir.dt.float8_e4m3fn_x4
FP4X4 = mybir.dt.float4_e2m1fn_x4
ALU = mybir.AluOpType
ACT = mybir.ActivationFunctionType

P = 128
PACK = 4
KP = 512
N = 512
DG = D // KP
JG = J // KP
HALVES = M // N
SCALED_BUFS = 6
SIG_BUFS = 16


def tile_shifted_mode_correction_h2_kernel(
    tc, x_words, x_scales, left_words, left_scales, right, lam, shift, start, row_scale, out_0, out_1, out_2
):
    nc = tc.nc
    with ExitStack() as ctx:
        keep = ctx.enter_context(tc.tile_pool(name="keep", bufs=1))
        work = ctx.enter_context(tc.tile_pool(name="work", bufs=1))
        psum = ctx.enter_context(tc.psum_pool(name="psum", bufs=8))
        ctx.enter_context(tc.manual_schedule())

        ident = keep.tile([P, P], F32, name="ident")
        warm = keep.tile([P, 2], F32, name="warm")
        lam_rows = keep.tile([P, JG * P], BF16, name="lam_rows")
        lam_rows32 = keep.tile([P, JG * P], F32, name="lam_rows32")
        ln_lam_rows = keep.tile([P, JG * P], F32, name="ln_lam_rows")
        shift_cols = keep.tile([P, HALVES, PACK], BF16, name="shift_cols")
        ln_shift_cols = keep.tile([P, HALVES * PACK], F32, name="ln_shift_cols")
        ln_lam = keep.tile([P, JG, PACK], F32, name="ln_lam")
        inv_lam = keep.tile([P, JG, PACK], F32, name="inv_lam")
        ln_shift = [keep.tile([P, N], F32, name="ln_shift%d" % h) for h in range(HALVES)]
        rs_raw = keep.tile([P, DG, PACK], BF16, name="rs_raw")
        rs32 = keep.tile([P, DG * PACK], F32, name="rs32")
        x_sc = keep.tile([P, DG, M], U8, name="x_sc", align_bytes=64)
        l_sc_raw = work.tile([P, DG, J], U8, name="l_sc_raw", tag="grouped", bufs=3, align_bytes=64)
        l_sc = keep.tile([P, DG * J], U8, name="l_sc", align_bytes=64)
        l_raw = work.tile([P, DG, J // 2], I32, name="l_raw", tag="y32", bufs=3, align_bytes=64)
        l_codes = keep.tile([P, DG * J * 2], U8, name="l_codes", align_bytes=64)
        x_codes = [keep.tile([P, DG, N], U32, name="x_codes%d" % h, align_bytes=64) for h in range(HALVES)]
        r_codes = keep.tile([P, JG, D], U32, name="r_codes", align_bytes=64)
        r_sc = keep.tile([P, JG, D], U8, name="r_sc", align_bytes=64)
        z_codes = keep.tile([P, JG, M], U32, name="z_codes", align_bytes=64)
        z_sc = keep.tile([P, JG, M], U8, name="z_sc", align_bytes=64)
        y_sc = keep.tile([P, M], U8, name="y_sc", align_bytes=64)

        live = {}

        def half(h):
            return slice(h * N, (h + 1) * N)

        def load_right(jg, dh):
            rows = right[jg * KP : (jg + 1) * KP, dh * (D // 2) : (dh + 1) * (D // 2)]
            by_slot = rows.rearrange("(b t i) d -> t b i d", t=PACK, i=8)
            raw = work.tile([P, PACK, D // 2], BF16, name="r_raw", tag="rows", bufs=6)
            for t in range(PACK):
                nc.sync.dma_start(out=raw[:, t, :], in_=by_slot[t])
            live["raw", jg, dh] = raw

        def load_scales(plane, rows):
            for q in range(4):
                src = rows[:, 4 * q : 4 * q + 4, :].rearrange("g r n -> r g n")
                nc.sync.dma_start(out=plane[32 * q : 32 * q + 4, :, :].bitcast(I32), in_=src.bitcast(I32))

        def load_left():
            nc.sync.dma_start(out=l_raw[:], in_=left_words.rearrange("g p n -> p g n").bitcast(I32))

        def load_x(h):
            src = x_words.rearrange("g p n t -> p g (n t)")[:, :, h * N * 4 : (h + 1) * N * 4]
            nc.sync.dma_start(out=x_codes[h][:].bitcast(I32), in_=src.bitcast(I32))

        def load_start(g):
            src = start[g * KP : (g + 1) * KP, :].rearrange("(p t) m -> p t m", t=PACK)
            rows = work.tile([P, PACK, M], BF16, name="start_rows", tag="rows", bufs=6)
            nc.sync.dma_start(out=rows[:], in_=src)
            live["start", g] = rows

        def interleave(engine, grouped, rows):
            dst = grouped[:].rearrange("p (c i t) -> p c t i", i=4, t=PACK)
            src = rows.rearrange("p t (c i) -> p c t i", i=4)
            if engine == "vector":
                nc.vector.tensor_copy(out=dst, in_=src)
            else:
                nc.scalar.copy(out=dst, in_=src)

        def group_right(jg, g, engine):
            grouped = work.tile([P, KP * PACK], BF16, name="r_grouped", tag="r_grouped", bufs=2, align_bytes=64)
            cols = slice((g % 2) * KP, (g % 2 + 1) * KP)
            dst = grouped[:].rearrange("p (t m j) -> p m j t", t=PACK, j=PACK)
            src = live["raw", jg, g // 2][:, :, cols].rearrange("p j (m t) -> p m j t", t=PACK)
            if engine == "vector":
                nc.vector.tensor_copy(out=dst, in_=src)
            else:
                nc.scalar.copy(out=dst, in_=src)
            live["r", jg, g] = grouped

        def quantize_right(jg, g):
            cols = slice(g * KP, (g + 1) * KP)
            nc.vector.quantize_mx(
                out=r_codes[:, jg, cols].bitcast(FP8X4), scales=r_sc[:, jg, cols], in_=live["r", jg, g][:]
            )

        def permute_left_scales():
            dst = l_sc[:].bitcast(I32).rearrange("p (a t b w) -> p a t b w", t=PACK, b=16, w=2)
            src = l_sc_raw[:].rearrange("p g n -> p (g n)").bitcast(I32)
            src = src.rearrange("p (a b t w) -> p a b t w", t=PACK, b=16, w=2)
            nc.vector.tensor_copy(out=dst, in_=src.rearrange("p a b t w -> p a t b w"))

        def permute_left_codes():
            dst = l_codes[:].bitcast(I32).rearrange("p (a t b w) -> p a t b w", t=PACK, b=16, w=4)
            src = l_raw[:].rearrange("p g n -> p (g n)").rearrange("p (a b t w) -> p a b t w", t=PACK, b=16, w=4)
            nc.vector.tensor_copy(out=dst, in_=src.rearrange("p a b t w -> p a t b w"))

        def weight(h, jg, t):
            sig = work.tile([P, N], F32, name="sig", tag="sig", bufs=SIG_BUFS)
            nc.scalar.activation(
                out=sig[:], in_=ln_shift[h][:], func=ACT.Sigmoid, scale=-1.0, bias=ln_lam[:, jg, t : t + 1]
            )
            live["sig", h, jg, t] = sig

        def project(h, jg, t):
            bank = psum.tile([P, N], F32, name="bank", tag="bank")
            for g in range(DG):
                col = g * J + jg * KP + t * P
                nc.tensor.matmul_mx(
                    out=bank[:],
                    lhsT=l_codes[:, 2 * col : 2 * (col + P)].bitcast(FP4X4),
                    lhsT_scale=l_sc[:, col : col + P],
                    rhs=x_codes[h][:, g, :].bitcast(FP8X4),
                    rhs_scale=x_sc[:, g, half(h)],
                    start=(g == 0),
                    stop=(g == DG - 1),
                )
            live["c", h, jg, t] = bank

        def divide(h, jg, t):
            if t == 0:
                live["z", h, jg] = work.tile([P, PACK, N], BF16, name="z_rows", tag="z_rows", bufs=2)
            nc.vector.scalar_tensor_tensor(
                out=live["z", h, jg][:, t, :],
                in0=live["c", h, jg, t][:],
                scalar=inv_lam[:, jg, t : t + 1],
                in1=live["sig", h, jg, t][:],
                op0=ALU.mult,
                op1=ALU.mult,
            )

        def group_z(h, jg, engine):
            grouped = work.tile([P, N * PACK], BF16, name="z_grouped", tag="grouped", bufs=3, align_bytes=64)
            interleave(engine, grouped, live["z", h, jg][:])
            live["zg", h, jg] = grouped

        def quantize_z(h, jg):
            nc.vector.quantize_mx(
                out=z_codes[:, jg, half(h)].bitcast(FP8X4), scales=z_sc[:, jg, half(h)], in_=live["zg", h, jg][:]
            )

        def scale_start(tile, t, engine):
            g, c0, width = tile
            scaled = work.tile([P, width], F32, name="scaled", tag="scaled", bufs=SCALED_BUFS)
            col = g * PACK + t
            src = live["start", g][:, t, c0 : c0 + width]
            if engine == "scalar":
                nc.scalar.activation(out=scaled[:], in_=src, func=ACT.Copy, scale=rs32[:, col : col + 1])
            elif engine == "vector":
                nc.vector.tensor_scalar(
                    out=scaled[:], in0=src, scalar1=rs32[:, col : col + 1], scalar2=None, op0=ALU.mult
                )
            else:
                nc.gpsimd.tensor_scalar(
                    out=scaled[:], in0=src, scalar1=rs32[:, col : col + 1], scalar2=0.0, op0=ALU.mult, op1=ALU.add
                )
            live["s", tile, t] = scaled

        def expand(tile, t):
            g, c0, width = tile
            bank = psum.tile([P, width], F32, name="bank", tag="bank")
            cols = slice(g * KP + t * P, g * KP + (t + 1) * P)
            for jg in range(JG):
                nc.tensor.matmul_mx(
                    out=bank[:],
                    lhsT=r_codes[:, jg, cols].bitcast(FP8X4),
                    lhsT_scale=r_sc[:, jg, cols],
                    rhs=z_codes[:, jg, c0 : c0 + width].bitcast(FP8X4),
                    rhs_scale=z_sc[:, jg, c0 : c0 + width],
                    start=(jg == 0),
                    stop=(jg == JG - 1),
                )
            live["v", tile, t] = bank

        def correct(tile, t):
            g, c0, width = tile
            if t == 0:
                live["y", tile] = work.tile([P, PACK, width], F32, name="y32", tag="y32", bufs=3, align_bytes=64)
            col = g * PACK + t
            nc.vector.scalar_tensor_tensor(
                out=live["y", tile][:, t, :],
                in0=live["v", tile, t][:],
                scalar=rs32[:, col : col + 1],
                in1=live["s", tile, t][:],
                op0=ALU.mult,
                op1=ALU.add,
            )

        def store_y(tile):
            g, c0, width = tile
            dst = out_0[g * KP : (g + 1) * KP, c0 : c0 + width].rearrange("(p t) m -> p t m", t=PACK)
            nc.sync.dma_start(out=dst, in_=live["y", tile][:])

        def group_y(tile, engine):
            g, c0, width = tile
            grouped = work.tile([P, width * PACK], BF16, name="y_grouped", tag="grouped", bufs=3, align_bytes=64)
            interleave(engine, grouped, live["y", tile][:])
            live["yg", tile] = grouped

        def quantize_y(tile):
            g, c0, width = tile
            codes = work.tile([P, width], U32, name="y_codes", tag="y_codes", bufs=3, align_bytes=64)
            nc.vector.quantize_mx(
                out=codes[:].bitcast(FP8X4), scales=y_sc[4 * g : P, c0 : c0 + width], in_=live["yg", tile][:]
            )
            dst = out_1[g].rearrange("p m t -> p (m t)")[:, c0 * 4 : (c0 + width) * 4]
            nc.sync.dma_start(out=dst.bitcast(I32), in_=codes[:].bitcast(I32))

        def store_y_scales(h):
            for q in range(4):
                dst = out_2[:, 4 * q : 4 * q + 4, half(h)]
                nc.sync.dma_start(out=dst.bitcast(I32), in_=y_sc[32 * q : 32 * q + 16, half(h)].bitcast(I32))

        def prologue_memsets():
            nc.vector.memset(warm[:], 1.0)
            nc.vector.memset(lam_rows[:], 1.0)
            nc.scalar.activation(out=warm[:, 1:2], in_=warm[:, 0:1], func=ACT.Ln)
            make_identity(nc, ident[:])
            nc.vector.memset(l_sc_raw[:].rearrange("p g n -> p (g n)").bitcast(I32), 0)
            nc.vector.memset(x_sc[:].rearrange("p g n -> p (g n)").bitcast(I32), 0)

        def load_small():
            nc.sync.dma_start(out=shift_cols[:], in_=shift.rearrange("(h p c) -> p h c", h=HALVES, c=PACK))
            nc.sync.dma_start(
                out=lam_rows[0:PACK, :].rearrange("t (b i) -> t b i", i=8),
                in_=lam.rearrange("(b t i) -> t b i", t=PACK, i=8),
            )

        def load_rs():
            nc.sync.dma_start(out=rs_raw[:], in_=row_scale.rearrange("(g p t) -> p g t", g=DG, t=PACK))
            nc.gpsimd.tensor_copy(out=rs32[:], in_=rs_raw[:].rearrange("p g t -> p (g t)"))

        def spread_shift(h):
            spread = psum.tile([P, PACK, P], F32, name="spread", tag="bank")
            for c in range(PACK):
                col = h * PACK + c
                nc.tensor.transpose(spread[:, c, :], ln_shift_cols[:, col : col + 1].to_broadcast([P, P]), ident[:])
            nc.vector.tensor_copy(
                out=ln_shift[h][:].rearrange("p (n c) -> p n c", c=PACK), in_=spread[:].rearrange("p c n -> p n c")
            )

        def turn(rows):
            turned = psum.tile([P, JG, P], F32, name="turned", tag="bank")
            for jg in range(JG):
                nc.tensor.transpose(turned[:, jg, :], rows[:, jg * P : (jg + 1) * P], ident[:])
            return turned[:, :, 0:PACK]

        def logs():
            nc.scalar.activation(out=ln_shift_cols[:], in_=shift_cols[:].rearrange("p h c -> p (h c)"), func=ACT.Ln)
            nc.scalar.activation(out=ln_lam_rows[:], in_=lam_rows[:], func=ACT.Ln)
            nc.scalar.activation(out=warm[:, 1:2], in_=warm[:, 0:1], func=ACT.Sigmoid)
            nc.vector.tensor_copy(out=lam_rows32[:], in_=lam_rows[:])
            spread_shift(0)
            nc.vector.tensor_copy(out=ln_lam[:], in_=turn(ln_lam_rows))
            spread_shift(1)
            nc.vector.reciprocal(out=inv_lam[:], in_=turn(lam_rows32))


        V, S, G = "vector", "scalar", "gpsimd"
        tiles = [(g, 0, N) for g in range(DG)] + [(g, N, N) for g in range(DG - 1)]
        tiles += [(DG - 1, N, N // 2), (DG - 1, N + N // 2, N // 2)]
        start_engine = [[G] * 4] * 9

        prologue_memsets()
        load_small()
        load_left()
        load_right(0, 0)
        load_scales(l_sc_raw, left_scales)
        load_scales(x_sc, x_scales)
        load_x(0)
        load_rs()
        load_right(1, 0)
        load_right(0, 1)
        load_start(0)
        load_x(1)
        load_right(1, 1)
        load_start(1)
        logs()
        permute_left_codes()
        group_right(0, 0, V)
        permute_left_scales()
        group_right(0, 1, V)
        quantize_right(0, 0)
        quantize_right(0, 1)
        load_start(2)
        units = [(h, jg, t) for h in range(HALVES) for jg in range(JG) for t in range(PACK)]
        for unit in units[:14]:
            weight(*unit)
        for unit in units[:8]:
            project(*unit)
        divide(0, 0, 0)
        group_right(1, 0, V)
        group_right(1, 1, S)
        load_start(3)
        divide(0, 0, 1)
        quantize_right(1, 0)
        group_right(0, 2, S)
        divide(0, 0, 2)
        quantize_right(1, 1)
        divide(0, 0, 3)
        group_z(0, 0, S)
        for unit in units[8:12]:
            project(*unit)
        divide(0, 1, 0)
        divide(0, 1, 1)
        quantize_right(0, 2)
        group_right(0, 3, S)
        divide(0, 1, 2)
        divide(0, 1, 3)
        quantize_z(0, 0)
        group_z(0, 1, V)
        divide(1, 0, 0)
        quantize_z(0, 1)
        divide(1, 0, 1)
        quantize_right(0, 3)
        for unit in units[14:]:
            weight(*unit)
        group_right(1, 2, S)
        divide(1, 0, 2)
        divide(1, 0, 3)

        def tile_front(i):
            for t in range(PACK):
                scale_start(tiles[i], t, start_engine[i][t])
                expand(tiles[i], t)

        def tile_back(i, between):
            for t in range(PACK):
                correct(tiles[i], t)
                if t == PACK - 1:
                    store_y(tiles[i])
                for step in between.get(t, []):
                    step[0](*step[1:])

        tile_front(0)
        tile_back(0, {1: [(quantize_right, 1, 2), (group_right, 1, 3, S)]})
        tile_front(1)
        project(1, 1, 0)
        project(1, 1, 1)
        group_y(tiles[0], S)
        group_z(1, 0, S)
        tile_back(1, {1: [(quantize_right, 1, 3)], 3: [(divide, 1, 1, 0), (quantize_y, tiles[0]), (divide, 1, 1, 1)]})
        project(1, 1, 2)
        project(1, 1, 3)
        tile_front(2)
        group_y(tiles[1], S)
        divide(1, 1, 2)
        divide(1, 1, 3)
        group_z(1, 1, S)
        tile_back(2, {0: [(quantize_z, 1, 0)], 2: [(quantize_y, tiles[1])]})
        tile_front(3)
        group_y(tiles[2], S)
        tile_back(3, {0: [(quantize_z, 1, 1)], 3: [(quantize_y, tiles[2])]})
        for i in range(4, len(tiles)):
            tile_front(i)
            group_y(tiles[i - 1], S)
            tile_back(i, {3: [(quantize_y, tiles[i - 1])]} if i < 7 else {})
            if i == 4:
                store_y_scales(0)
        quantize_y(tiles[-3])
        group_y(tiles[-1], V)
        quantize_y(tiles[-2])
        quantize_y(tiles[-1])
        store_y_scales(1)
